import numpy as np
import ml_dtypes

BF16 = ml_dtypes.bfloat16


def bf(x):
    return np.asarray(x, np.float32).astype(BF16)


def f32(x):
    return np.asarray(x, np.float32)


def f64(x):
    return np.asarray(x).astype(np.float64)


def striped(idx):
    return np.concatenate([l.reshape(-1, 16).T for l in idx])


def rows(idx, k):
    return np.tile(np.repeat(idx, 16, axis=0), (k // (16 * 8), 1))


def look(tab, idx):
    return np.take_along_axis(f64(tab), rows(idx, len(tab)), axis=1)


K, S, D, V, N, M = 512, 2048, 3, 512, 1536, 512


def setup_inputs():
    return {"tab": bf(np.random.standard_normal((K, S))), "u": bf(np.random.uniform(0.2, 1.0, (D, K, V))), "w": bf(np.random.standard_normal((K, M)) / np.sqrt(K)), "b": f32(0.5 * np.random.standard_normal((M, 1))), "offs": striped(np.stack([np.random.permutation(S)[:N] for _ in range(8)]))}


def reference(tab, u, w, b, offs):
    idx = np.stack([g.T.reshape(-1) for g in np.split(offs, 8)])
    x = sum(f64(u[d]) * look(tab, idx[:, d * V:(d + 1) * V]) for d in range(D))
    y = f64(w).T @ x
    return np.maximum(y + f64(b), 0.0)

@@ -1,0 +1,89 @@
+import concourse.mybir as mybir
+
+BF16 = mybir.dt.bfloat16
+F32 = mybir.dt.float32
+U16 = mybir.dt.uint16
+ADD = mybir.AluOpType.add
+MAX = mybir.AluOpType.max
+MULT = mybir.AluOpType.mult
+RELU = mybir.ActivationFunctionType.Relu
+
+P = 128
+ROWS, PLACES = 512, 2048
+D, COLS = 3, 512
+M = 512
+ROW_BLOCKS = ROWS // P
+M_BLOCKS = M // P
+LIST_COLS = COLS // 16
+BIAS_ROWS = 32
+
+FLOPS = 2 * D * ROWS * COLS + 2 * ROWS * M * COLS
+
+
+def tile_lookup_mix_mul_relu_kernel(tc, tab, u, w, b, offs, out):
+    nc = tc.nc
+    with (
+        tc.tile_pool(name="held", bufs=1) as held,
+        tc.tile_pool(name="products", bufs=4) as products,
+        tc.tile_pool(name="results", bufs=M_BLOCKS) as results,
+        tc.psum_pool(name="psum", bufs=1) as psum,
+    ):
+        offsets = held.tile([P, D * LIST_COLS], U16, name="offsets")
+        nc.sync.dma_start(offsets[:], offs)
+
+        tables, factors, layers = [], [], []
+        for k in range(ROW_BLOCKS):
+            rows = slice(k * P, (k + 1) * P)
+            table = held.tile([P, PLACES], BF16, name=f"table{k}")
+            nc.sync.dma_start(table[:], tab[rows, :])
+            factor = held.tile([P, D, COLS], BF16, name=f"factor{k}")
+            nc.sync.dma_start(factor[:], u[:, rows, :].rearrange("d r j -> r d j"))
+            layer = held.tile([P, M], BF16, name=f"layer{k}")
+            nc.sync.dma_start(layer[:], w[rows, :])
+            tables.append(table)
+            factors.append(factor)
+            layers.append(layer)
+
+        bias_row = held.tile([BIAS_ROWS, M], F32, name="bias_row")
+        nc.gpsimd.memset(bias_row[:], 0.0)
+        nc.scalar.dma_start(bias_row[0:1, :], b.rearrange("m o -> o m"))
+        ones = held.tile([BIAS_ROWS, 1], F32, name="ones")
+        nc.gpsimd.memset(ones[:], 1.0)
+        bias_psum = psum.tile([P, M_BLOCKS], F32, name="bias_psum")
+        for m in range(M_BLOCKS):
+            nc.tensor.matmul(
+                bias_psum[:, m : m + 1],
+                bias_row[:, m * P : (m + 1) * P],
+                ones[:],
+                start=True,
+                stop=True,
+            )
+        bias = held.tile([P, M_BLOCKS], F32, name="bias")
+        nc.scalar.copy(bias[:], bias_psum[:])
+
+        sums = [psum.tile([P, COLS], F32, name=f"sum{m}") for m in range(M_BLOCKS)]
+        for k in range(ROW_BLOCKS):
+            for d in range(D):
+                product = products.tile([P, COLS], BF16, name="product")
+                places = offsets[:, d * LIST_COLS : (d + 1) * LIST_COLS]
+                nc.vector.tensor_tensor(
+                    product[:], tables[k][:].indirect(places), factors[k][:, d, :], MULT
+                )
+                for m in range(M_BLOCKS):
+                    nc.tensor.matmul(
+                        sums[m][:],
+                        layers[k][:, m * P : (m + 1) * P],
+                        product[:],
+                        start=(k == 0 and d == 0),
+                        stop=(k == ROW_BLOCKS - 1 and d == D - 1),
+                    )
+
+        for m in range(M_BLOCKS):
+            result = results.tile([P, COLS], F32, name="result")
+            if m % 2 == 0:
+                nc.scalar.activation(result[:], sums[m][:], RELU, bias=bias[:, m : m + 1])
+            else:
+                nc.vector.tensor_scalar(
+                    result[:], sums[m][:], bias[:, m : m + 1], 0.0, ADD, MAX
+                )
+            nc.sync.dma_start(out[m * P : (m + 1) * P, :], result[:])

@@ -15,7 +15,6 @@ M = 512
 ROW_BLOCKS = ROWS // P
 M_BLOCKS = M // P
 LIST_COLS = COLS // 16
-BIAS_ROWS = 32
 
 FLOPS = 2 * D * ROWS * COLS + 2 * ROWS * M * COLS
 
@@ -24,37 +23,38 @@ def tile_lookup_mix_mul_relu_kernel(tc, tab, u, w, b, offs, out):
     nc = tc.nc
     with (
         tc.tile_pool(name="held", bufs=1) as held,
-        tc.tile_pool(name="products", bufs=4) as products,
+        tc.tile_pool(name="products", bufs=ROW_BLOCKS * D) as products,
         tc.tile_pool(name="results", bufs=M_BLOCKS) as results,
         tc.psum_pool(name="psum", bufs=1) as psum,
     ):
         offsets = held.tile([P, D * LIST_COLS], U16, name="offsets")
         nc.sync.dma_start(offsets[:], offs)
 
+        bias_row = held.tile([1, M], F32, name="bias_row")
+        nc.scalar.dma_start(bias_row[:], b.rearrange("m o -> o m"))
+
         tables, factors, layers = [], [], []
         for k in range(ROW_BLOCKS):
             rows = slice(k * P, (k + 1) * P)
             table = held.tile([P, PLACES], BF16, name=f"table{k}")
             nc.sync.dma_start(table[:], tab[rows, :])
-            factor = held.tile([P, D, COLS], BF16, name=f"factor{k}")
-            nc.sync.dma_start(factor[:], u[:, rows, :].rearrange("d r j -> r d j"))
+            for d in range(D):
+                factor = held.tile([P, COLS], BF16, name=f"factor{k}_{d}")
+                nc.sync.dma_start(factor[:], u[d, rows, :])
+                factors.append(factor)
             layer = held.tile([P, M], BF16, name=f"layer{k}")
             nc.sync.dma_start(layer[:], w[rows, :])
             tables.append(table)
-            factors.append(factor)
             layers.append(layer)
 
-        bias_row = held.tile([BIAS_ROWS, M], F32, name="bias_row")
-        nc.gpsimd.memset(bias_row[:], 0.0)
-        nc.scalar.dma_start(bias_row[0:1, :], b.rearrange("m o -> o m"))
-        ones = held.tile([BIAS_ROWS, 1], F32, name="ones")
-        nc.gpsimd.memset(ones[:], 1.0)
+        one = held.tile([1, 1], F32, name="one")
+        nc.gpsimd.memset(one[:], 1.0)
         bias_psum = psum.tile([P, M_BLOCKS], F32, name="bias_psum")
         for m in range(M_BLOCKS):
             nc.tensor.matmul(
                 bias_psum[:, m : m + 1],
                 bias_row[:, m * P : (m + 1) * P],
-                ones[:],
+                one[:],
                 start=True,
                 stop=True,
             )
@@ -67,7 +67,10 @@ def tile_lookup_mix_mul_relu_kernel(tc, tab, u, w, b, offs, out):
                 product = products.tile([P, COLS], BF16, name="product")
                 places = offsets[:, d * LIST_COLS : (d + 1) * LIST_COLS]
                 nc.vector.tensor_tensor(
-                    product[:], tables[k][:].indirect(places), factors[k][:, d, :], MULT
+                    product[:],
+                    tables[k][:].indirect(places),
+                    factors[k * D + d][:],
+                    MULT,
                 )
                 for m in range(M_BLOCKS):
                     nc.tensor.matmul(

@@ -12,6 +12,7 @@ P = 128
 ROWS, PLACES = 512, 2048
 D, COLS = 3, 512
 M = 512
+HALF = COLS // 2
 ROW_BLOCKS = ROWS // P
 M_BLOCKS = M // P
 LIST_COLS = COLS // 16
@@ -24,7 +25,7 @@ def tile_lookup_mix_mul_relu_kernel(tc, tab, u, w, b, offs, out):
     with (
         tc.tile_pool(name="held", bufs=1) as held,
         tc.tile_pool(name="products", bufs=ROW_BLOCKS * D) as products,
-        tc.tile_pool(name="results", bufs=M_BLOCKS) as results,
+        tc.tile_pool(name="results", bufs=2 * M_BLOCKS) as results,
         tc.psum_pool(name="psum", bufs=1) as psum,
     ):
         offsets = held.tile([P, D * LIST_COLS], U16, name="offsets")
@@ -82,11 +83,14 @@ def tile_lookup_mix_mul_relu_kernel(tc, tab, u, w, b, offs, out):
                     )
 
         for m in range(M_BLOCKS):
-            result = results.tile([P, COLS], F32, name="result")
-            if m % 2 == 0:
-                nc.scalar.activation(result[:], sums[m][:], RELU, bias=bias[:, m : m + 1])
-            else:
-                nc.vector.tensor_scalar(
-                    result[:], sums[m][:], bias[:, m : m + 1], 0.0, ADD, MAX
-                )
-            nc.sync.dma_start(out[m * P : (m + 1) * P, :], result[:])
+            bias_m = bias[:, m : m + 1]
+            for half in range(2):
+                cols = slice(half * HALF, (half + 1) * HALF)
+                result = results.tile([P, HALF], F32, name="result")
+                if m % 2 == 0:
+                    nc.scalar.activation(result[:], sums[m][:, cols], RELU, bias=bias_m)
+                else:
+                    nc.vector.tensor_scalar(
+                        result[:], sums[m][:, cols], bias_m, 0.0, ADD, MAX
+                    )
+                nc.sync.dma_start(out[m * P : (m + 1) * P, cols], result[:])

import concourse.mybir as mybir

BF16 = mybir.dt.bfloat16
F32 = mybir.dt.float32
U16 = mybir.dt.uint16
ADD = mybir.AluOpType.add
MAX = mybir.AluOpType.max
MULT = mybir.AluOpType.mult
RELU = mybir.ActivationFunctionType.Relu

P = 128
ROWS, PLACES = 512, 2048
D, COLS = 3, 512
M = 512
HALF = COLS // 2
ROW_BLOCKS = ROWS // P
M_BLOCKS = M // P
LIST_COLS = COLS // 16

FLOPS = 2 * D * ROWS * COLS + 2 * ROWS * M * COLS


def tile_lookup_mix_mul_relu_kernel(tc, tab, u, w, b, offs, out):
    nc = tc.nc
    with (
        tc.tile_pool(name="held", bufs=1) as held,
        tc.tile_pool(name="products", bufs=ROW_BLOCKS * D) as products,
        tc.tile_pool(name="results", bufs=2 * M_BLOCKS) as results,
        tc.psum_pool(name="psum", bufs=1) as psum,
    ):
        offsets = held.tile([P, D * LIST_COLS], U16, name="offsets")
        nc.sync.dma_start(offsets[:], offs)

        bias_row = held.tile([1, M], F32, name="bias_row")
        nc.scalar.dma_start(bias_row[:], b.rearrange("m o -> o m"))

        tables, factors, layers = [], [], []
        for k in range(ROW_BLOCKS):
            rows = slice(k * P, (k + 1) * P)
            table = held.tile([P, PLACES], BF16, name=f"table{k}")
            nc.sync.dma_start(table[:], tab[rows, :])
            for d in range(D):
                factor = held.tile([P, COLS], BF16, name=f"factor{k}_{d}")
                nc.sync.dma_start(factor[:], u[d, rows, :])
                factors.append(factor)
            layer = held.tile([P, M], BF16, name=f"layer{k}")
            nc.sync.dma_start(layer[:], w[rows, :])
            tables.append(table)
            layers.append(layer)

        one = held.tile([1, 1], F32, name="one")
        nc.gpsimd.memset(one[:], 1.0)
        bias_psum = psum.tile([P, M_BLOCKS], F32, name="bias_psum")
        for m in range(M_BLOCKS):
            nc.tensor.matmul(
                bias_psum[:, m : m + 1],
                bias_row[:, m * P : (m + 1) * P],
                one[:],
                start=True,
                stop=True,
            )
        bias = held.tile([P, M_BLOCKS], F32, name="bias")
        nc.scalar.copy(bias[:], bias_psum[:])

        sums = [psum.tile([P, COLS], F32, name=f"sum{m}") for m in range(M_BLOCKS)]
        for k in range(ROW_BLOCKS):
            for d in range(D):
                product = products.tile([P, COLS], BF16, name="product")
                places = offsets[:, d * LIST_COLS : (d + 1) * LIST_COLS]
                nc.vector.tensor_tensor(
                    product[:],
                    tables[k][:].indirect(places),
                    factors[k * D + d][:],
                    MULT,
                )
                for m in range(M_BLOCKS):
                    nc.tensor.matmul(
                        sums[m][:],
                        layers[k][:, m * P : (m + 1) * P],
                        product[:],
                        start=(k == 0 and d == 0),
                        stop=(k == ROW_BLOCKS - 1 and d == D - 1),
                    )

        for m in range(M_BLOCKS):
            bias_m = bias[:, m : m + 1]
            for half in range(2):
                cols = slice(half * HALF, (half + 1) * HALF)
                result = results.tile([P, HALF], F32, name="result")
                if m % 2 == 0:
                    nc.scalar.activation(result[:], sums[m][:, cols], RELU, bias=bias_m)
                else:
                    nc.vector.tensor_scalar(
                        result[:], sums[m][:, cols], bias_m, 0.0, ADD, MAX
                    )
                nc.sync.dma_start(out[m * P : (m + 1) * P, cols], result[:])
